import numpy as np
import ml_dtypes


def mxq(x, axis, fmt="e4m3"):
    dtype, down = {"e4m3": (ml_dtypes.float8_e4m3fn, 7), "e5m2": (ml_dtypes.float8_e5m2, 14)}[fmt]
    v = np.moveaxis(np.asarray(x, np.float32).astype(ml_dtypes.bfloat16).astype(np.float64), axis, -1)
    blocks = v.reshape(v.shape[:-1] + (-1, 32))
    amax = np.abs(blocks).max(-1, keepdims=True)
    byte = np.maximum(np.where(amax > 0, np.frexp(amax)[1] - 1 + 127, 0) - down, 1)
    scale = np.exp2(byte - 127.0)
    codes = (blocks / scale).astype(np.float32).astype(dtype).astype(np.float64)
    return np.moveaxis((codes * scale).reshape(v.shape), -1, axis)


WIDE = False


def mx_kscale(k):
    if not WIDE:
        return np.ones(k)
    levels = np.array([24, -24, 12, -12, 0])
    if k % 512:
        return np.exp2(np.random.permutation(np.resize(levels, k // 32))).repeat(32)
    a = np.empty((k // 512, 16))
    for p in range(k // 512):
        a[p, :8] = np.random.permutation(np.resize(levels, 8))
        for g in range(8):
            far = levels[np.abs(levels - a[p, g]) >= 10]
            a[p, g + 8] = far[np.random.randint(len(far))]
    return np.exp2(a.ravel()).repeat(32)


def f64(x):
    return np.asarray(x).astype(np.float64)


def striped8(idx):
    return np.concatenate([v.reshape(-1, 16).T for v in idx]).astype(np.uint16)


def unstriped8(offs):
    return np.stack([offs[16 * g:16 * g + 16].T.reshape(-1) for g in range(8)]).astype(np.int64)


E2M1 = np.array([0.0, 0.5, 1.0, 1.5, 2.0, 3.0, 4.0, 6.0, -0.0, -0.5, -1.0, -1.5, -2.0, -3.0, -4.0, -6.0])


def pack_weight(w, fmt):
    k, n = w.shape
    w = f64(np.asarray(w, np.float32).astype(ml_dtypes.bfloat16)).reshape(k // 32, 32, n)
    amax = np.abs(w).max(1)
    if fmt == "e4m3":
        byte = np.frexp(amax)[1] - 1 + 127 - 7
    else:
        mant, ex = np.frexp(amax / 6.0)
        byte = np.where(mant > 0.5, ex, ex - 1) + 127
    byte = np.clip(np.where(amax > 0, byte, 1), 1, 254)
    scaled = (w * np.exp2(127.0 - byte)[:, None, :]).reshape(k, n).astype(np.float32)
    by_word = np.ascontiguousarray(scaled.reshape(k // 512, 128, 4, n).transpose(0, 1, 3, 2))
    if fmt == "e4m3":
        words = by_word.astype(ml_dtypes.float8_e4m3fn).view(np.uint8)
    else:
        c = by_word.astype(ml_dtypes.float4_e2m1fn).view(np.uint8) & 0xF
        words = (c[..., 0::2] | (c[..., 1::2] << 4)).reshape(k // 512, 128, 2 * n)
    return np.ascontiguousarray(words), np.ascontiguousarray(byte.astype(np.uint8).reshape(k // 512, 16, n))


def unpack_weight(words, scales, fmt):
    g, _, n = scales.shape
    words = np.ascontiguousarray(words).reshape(g, 128, n, -1)
    if fmt == "e4m3":
        vals = words.view(ml_dtypes.float8_e4m3fn).astype(np.float64)
    else:
        nib = np.empty((g, 128, n, 4), np.uint8)
        nib[..., 0::2] = words & 0xF
        nib[..., 1::2] = words >> 4
        vals = E2M1[nib]
    vals = vals * np.repeat(np.exp2(scales.astype(np.float64) - 127.0), 8, axis=1)[..., None]
    return vals.transpose(0, 1, 3, 2).reshape(g * 512, n)


def silu(f):
    return f / (1.0 + np.exp(-np.maximum(f, -700.0)))


K, N, T, J = 1024, 512, 2048, 1024


def setup_inputs():
    n = np.random.standard_normal
    s = mx_kscale(K)[:, None]
    p_wk = pack_weight(n((K, N)) / np.sqrt(K) / s, "e4m3")
    p_wv4 = pack_weight(n((K, N)) / np.sqrt(K) / s, "e2m1")
    return {
        "xT": (n((K, T)) * s).astype(np.float32),
        "wgt": np.repeat(np.random.uniform(0.5, 2.0, (8, J)), 16, axis=0).astype(np.float32),
        "wk_words": p_wk[0],
        "wk_scales": p_wk[1],
        "wv4_words": p_wv4[0],
        "wv4_scales": p_wv4[1],
        "wvd": (0.4 * (n((K, N)) / np.sqrt(K) / s)).astype(np.float32),
        "st": (n((N, J))).astype(np.float32),
        "offs": striped8(np.stack([np.random.permutation(T)[:J] for _ in range(8)])),
    }


def reference(xT, wgt, wk_words, wk_scales, wv4_words, wv4_scales, wvd, st, offs):
    idx = unstriped8(offs)
    rows = np.arange(K)
    xg = f64(wgt)[rows // 4 % 128] * f64(xT)[rows[:, None], idx[rows % 512 // 64]]
    xT_ = mxq(xg, 0, "e4m3")
    wk_ = unpack_weight(wk_words, wk_scales, "e4m3")
    wv4_ = unpack_weight(wv4_words, wv4_scales, "e2m1")
    wvd_ = mxq(f64(wvd), 0, "e4m3")
    ke = wk_.T @ xT_
    ve = wv4_.T @ xT_ + wvd_.T @ xT_
    gate = silu(ke * f64(st))
    return gate * ve

@@ -1,0 +1,205 @@
+from contextlib import ExitStack
+
+import concourse.mybir as mybir
+
+K, N, T, J = 1024, 512, 2048, 1024
+FLOPS = 3 * 2 * K * N * J
+
+F32 = mybir.dt.float32
+BF16 = mybir.dt.bfloat16
+I32 = mybir.dt.int32
+U32 = mybir.dt.uint32
+U16 = mybir.dt.uint16
+U8 = mybir.dt.uint8
+FP8X4 = mybir.dt.float8_e4m3fn_x4
+FP4X4 = mybir.dt.float4_e2m1fn_x4
+MULT = mybir.AluOpType.mult
+SILU = mybir.ActivationFunctionType.Silu
+
+P = 128
+PACK = 4
+K_PASS = P * PACK
+PASSES = K // K_PASS
+HALF = 512
+HALVES = J // HALF
+N_TILES = N // P
+LIST_COLS = HALF // 16
+
+
+def interleave(copy, grouped, rows):
+    copy(
+        out=grouped.rearrange("p (c i) t -> p c t i", i=4),
+        in_=rows.rearrange("p t (c i) -> p c t i", i=4),
+    )
+
+
+def tile_list_dl_silu_kernel(
+    tc, xT, wgt, wk_words, wk_scales, wv4_words, wv4_scales, wvd, st, offs, out
+):
+    nc = tc.nc
+    with ExitStack() as ctx:
+        keep = ctx.enter_context(tc.tile_pool(name="keep", bufs=1))
+        ring = ctx.enter_context(tc.tile_pool(name="ring", bufs=4))
+        psum = ctx.enter_context(tc.psum_pool(name="psum", bufs=1))
+
+        offsets = keep.tile([P, J // 16], U16, name="offsets")
+        picked = {(a, h): keep.tile([P, PACK * HALF], F32, name=f"picked{a}{h}") for a in range(PASSES) for h in range(HALVES)}
+        wgt1 = keep.tile([P, HALF], F32, name="wgt1")
+        wgt_sb = [picked[1, 1][:, 3 * HALF // 2 : 5 * HALF // 2], wgt1[:]]
+        planes = [[keep.tile([P, T], F32, name=f"x{a}{i}") for i in range(PACK)] for a in range(PASSES)]
+        wk_codes = keep.tile([P, PASSES, N], U32, name="wk_codes", align_bytes=64)
+        wv4_codes = keep.tile([P, PASSES, 2 * N], U8, name="wv4_codes", align_bytes=64)
+        wk_sc = keep.tile([P, PASSES, N], U8, name="wk_sc", align_bytes=64)
+        wv4_sc = keep.tile([P, PASSES, N], U8, name="wv4_sc", align_bytes=64)
+        wvd_raw = [keep.tile([P, PACK, N], F32, name=f"wvd_raw{a}") for a in range(PASSES)]
+        st_sb = [[keep.tile([P, 2, HALF], F32, name=f"st{h}{u}") for u in range(2)] for h in range(HALVES)]
+
+        warm = keep.tile([P, 2], F32, name="warm")
+        nc.vector.memset(warm[:, 0:1], 0.0)
+        nc.scalar.activation(out=warm[:, 1:2], in_=warm[:, 0:1], func=SILU)
+        for plane in (wk_sc, wv4_sc):
+            nc.vector.memset(plane[:].rearrange("p a n -> p (a n)").bitcast(I32), 0)
+
+        def load_plane(a, i):
+            nc.sync.dma_start(out=planes[a][i][:], in_=xT[a * K_PASS + i : (a + 1) * K_PASS : PACK, :])
+
+        def load_scale_rows(plane, scales, r):
+            nc.sync.dma_start(
+                out=plane[r:P:32, :, :].bitcast(I32),
+                in_=scales[:, r:16:4, :].rearrange("a q n -> q a n").bitcast(I32),
+            )
+
+        nc.sync.dma_start(offsets[:], offs)
+        nc.sync.dma_start(out=wgt_sb[0], in_=wgt[:, 0:HALF])
+        load_plane(0, 0)
+        nc.sync.dma_start(out=wgt_sb[1], in_=wgt[:, HALF:J])
+        for i in range(1, PACK):
+            load_plane(0, i)
+        for i in range(PACK):
+            load_plane(1, i)
+            load_scale_rows(wk_sc, wk_scales, i)
+            load_scale_rows(wv4_sc, wv4_scales, i)
+        nc.sync.dma_start(
+            out=wk_codes[:].bitcast(I32), in_=wk_words.rearrange("a p n i -> p a (n i)").bitcast(I32)
+        )
+        nc.sync.dma_start(
+            out=wv4_codes[:].bitcast(I32), in_=wv4_words.rearrange("a p m -> p a m").bitcast(I32)
+        )
+        for a in range(PASSES):
+            nc.sync.dma_start(
+                out=wvd_raw[a][:],
+                in_=wvd[a * K_PASS : (a + 1) * K_PASS, :].rearrange("(p i) n -> p i n", i=PACK),
+            )
+        for h in range(HALVES):
+            for u in range(2):
+                nc.sync.dma_start(
+                    out=st_sb[h][u][:],
+                    in_=st[u * 2 * P : (u + 1) * 2 * P, h * HALF : (h + 1) * HALF].rearrange("(v p) j -> p v j", p=P),
+                )
+
+        grouped = {}
+        quantised = {}
+        for key in ("x00", "x01", "x10", "x11", "w0", "w1"):
+            grouped[key] = keep.tile([P, HALF, PACK], BF16, name=f"grouped_{key}", align_bytes=64)
+
+        def gather(a, i, h):
+            nc.vector.tensor_tensor(
+                picked[a, h][:, i * HALF : (i + 1) * HALF],
+                planes[a][i][:].indirect(offsets[:, h * LIST_COLS : (h + 1) * LIST_COLS]),
+                wgt_sb[h],
+                MULT,
+            )
+
+        def weave(a, h, first, last):
+            rows = picked[a, h][:, first * HALF : last * HALF].rearrange("p (t j) -> p t j", j=HALF)
+            interleave(nc.scalar.copy, grouped[f"x{a}{h}"][:, :, first:last], rows)
+
+        def quantise(key):
+            codes = keep.tile([P, HALF], U32, name=f"codes_{key}", align_bytes=64)
+            scales = keep.tile([P, HALF], U8, name=f"scales_{key}", align_bytes=64)
+            nc.vector.quantize_mx(
+                out=codes[:].bitcast(FP8X4), scales=scales[:], in_=grouped[key][:].rearrange("p w t -> p (w t)")
+            )
+            quantised[key] = (codes, scales)
+
+        for i in range(PACK):
+            for h in range(HALVES):
+                gather(0, i, h)
+        for h in range(HALVES):
+            weave(0, h, 0, 4)
+            quantise(f"x0{h}")
+        gather(1, 0, 0)
+        gather(1, 0, 1)
+        gather(1, 1, 0)
+        weave(1, 0, 0, 2)
+        gather(1, 2, 0)
+        gather(1, 3, 0)
+        weave(1, 0, 2, 4)
+        quantise("x10")
+        gather(1, 1, 1)
+        weave(1, 1, 0, 2)
+        gather(1, 2, 1)
+        gather(1, 3, 1)
+        weave(1, 1, 2, 4)
+        interleave(nc.vector.tensor_copy, grouped["w0"][:], wvd_raw[0][:])
+        quantise("w0")
+        quantise("x11")
+        interleave(nc.scalar.copy, grouped["w1"][:], wvd_raw[1][:])
+        quantise("w1")
+
+        def bank(b):
+            return psum.tile([P, HALF], F32, name=f"bank{b}")
+
+        def product(acc, which, t, a, h, start, stop):
+            cols = slice(t * P, (t + 1) * P)
+            if which == "wk":
+                codes, scales = wk_codes[:, a, cols].bitcast(FP8X4), wk_sc[:, a, cols]
+            elif which == "wv4":
+                codes, scales = wv4_codes[:, a, 2 * t * P : 2 * (t + 1) * P].bitcast(FP4X4), wv4_sc[:, a, cols]
+            else:
+                codes, scales = quantised[f"w{a}"][0][:, cols].bitcast(FP8X4), quantised[f"w{a}"][1][:, cols]
+            x_codes, x_scales = quantised[f"x{a}{h}"]
+            nc.tensor.matmul_mx(
+                out=acc[:], lhsT=codes, lhsT_scale=scales,
+                rhs=x_codes[:].bitcast(FP8X4), rhs_scale=x_scales[:],
+                start=start, stop=stop,
+            )
+
+        def make_gate(ke, t, h):
+            arg = ring.tile([P, HALF], F32, name="arg")
+            nc.vector.tensor_tensor(arg[:], ke[:], st_sb[h][t // 2][:, t % 2, :], MULT)
+            gate = ring.tile([P, HALF], F32, name="gate")
+            nc.scalar.activation(out=gate[:], in_=arg[:], func=SILU)
+            return gate
+
+        def finish(ve, gate, t, h):
+            res = ring.tile([P, HALF], F32, name="res")
+            nc.vector.tensor_tensor(res[:], ve[:], gate[:], MULT)
+            nc.sync.dma_start(out=out[t * P : (t + 1) * P, h * HALF : (h + 1) * HALF], in_=res[:])
+
+        tiles = range(N_TILES)
+        ke0 = [bank(t) for t in tiles]
+        ve0 = [bank(N_TILES + t) for t in tiles]
+        for a in range(PASSES):
+            for t in tiles:
+                product(ke0[t], "wk", t, a, 0, a == 0, a == 1)
+            for t in tiles:
+                product(ve0[t], "wv4", t, a, 0, a == 0, False)
+        for a in range(PASSES):
+            for t in tiles:
+                product(ve0[t], "wvd", t, a, 0, False, a == 1)
+        gates0 = [make_gate(ke0[t], t, 0) for t in tiles]
+        ke1 = []
+        for t in tiles:
+            finish(ve0[t], gates0[t], t, 0)
+            ke1.append(bank(N_TILES + t))
+            for a in range(PASSES):
+                product(ke1[t], "wk", t, a, 1, a == 0, a == 1)
+        ve1 = [bank(t) for t in tiles]
+        for t in tiles:
+            for which in ("wv4", "wvd"):
+                for a in range(PASSES):
+                    product(ve1[t], which, t, a, 1, which == "wv4" and a == 0, which == "wvd" and a == 1)
+        gates1 = [make_gate(ke1[t], t, 1) for t in tiles]
+        for t in tiles:
+            finish(ve1[t], gates1[t], t, 1)

@@ -43,15 +43,15 @@ def tile_list_dl_silu_kernel(
         psum = ctx.enter_context(tc.psum_pool(name="psum", bufs=1))
 
         offsets = keep.tile([P, J // 16], U16, name="offsets")
-        picked = {(a, h): keep.tile([P, PACK * HALF], F32, name=f"picked{a}{h}") for a in range(PASSES) for h in range(HALVES)}
-        wgt1 = keep.tile([P, HALF], F32, name="wgt1")
+        picked = {(a, h): keep.tile([P, 2560 if (a, h) == (1, 1) else PACK * HALF], F32, name=f"picked{a}{h}", align_bytes=64) for a in range(PASSES) for h in range(HALVES)}
+        wgt1 = keep.tile([P, HALF], F32, name="wgt1", align_bytes=64)
         wgt_sb = [picked[1, 1][:, 3 * HALF // 2 : 5 * HALF // 2], wgt1[:]]
         planes = [[keep.tile([P, T], F32, name=f"x{a}{i}") for i in range(PACK)] for a in range(PASSES)]
         wk_codes = keep.tile([P, PASSES, N], U32, name="wk_codes", align_bytes=64)
         wv4_codes = keep.tile([P, PASSES, 2 * N], U8, name="wv4_codes", align_bytes=64)
         wk_sc = keep.tile([P, PASSES, N], U8, name="wk_sc", align_bytes=64)
         wv4_sc = keep.tile([P, PASSES, N], U8, name="wv4_sc", align_bytes=64)
-        wvd_raw = [keep.tile([P, PACK, N], F32, name=f"wvd_raw{a}") for a in range(PASSES)]
+        wvd_raw = [keep.tile([P, PACK, N], F32, name=f"wvd_raw{a}")[:] for a in range(PASSES)]
         st_sb = [[keep.tile([P, 2, HALF], F32, name=f"st{h}{u}") for u in range(2)] for h in range(HALVES)]
 
         warm = keep.tile([P, 2], F32, name="warm")
@@ -69,38 +69,56 @@ def tile_list_dl_silu_kernel(
                 in_=scales[:, r:16:4, :].rearrange("a q n -> q a n").bitcast(I32),
             )
 
+        def load_wvd(a):
+            nc.sync.dma_start(
+                out=wvd_raw[a],
+                in_=wvd[a * K_PASS : (a + 1) * K_PASS, :].rearrange("(p i) n -> p i n", i=PACK),
+            )
+
+        def load_st(h, u):
+            nc.sync.dma_start(
+                out=st_sb[h][u][:],
+                in_=st[u * 2 * P : (u + 1) * 2 * P, h * HALF : (h + 1) * HALF].rearrange("(v p) j -> p v j", p=P),
+            )
+
         nc.sync.dma_start(offsets[:], offs)
-        nc.sync.dma_start(out=wgt_sb[0], in_=wgt[:, 0:HALF])
+        rows = keep.tile([P, 64], F32, name="wgt_rows", align_bytes=64)
+        for q in range(4):
+            nc.sync.dma_start(
+                out=rows[32 * q : 32 * (q + 1), :].rearrange("b (u c) -> b u c", u=2),
+                in_=wgt[32 * q : 32 * (q + 1) : 16, :].rearrange("u (b c) -> b u c", c=32),
+            )
+        turned = keep.tile([P, 64], F32, name="wgt_turned", align_bytes=64)
+        for u in range(2):
+            nc.vector.transpose(turned[:, 32 * u : 32 * (u + 1)], rows[:, 32 * u : 32 * (u + 1)])
+        for h in range(HALVES):
+            spread = keep.tile([P, HALF], F32, name=f"wgt_spread{h}", align_bytes=64)
+            nc.vector.tensor_copy(
+                out=spread[:].rearrange("p (b u r) -> p b u r", u=2, r=16),
+                in_=turned[:].rearrange("p (u b) -> p b u", u=2)[:, 16 * h : 16 * (h + 1), :].unsqueeze(3).to_broadcast([P, 16, 2, 16]),
+            )
+            nc.vector.transpose(wgt_sb[h], spread[:])
         load_plane(0, 0)
-        nc.sync.dma_start(out=wgt_sb[1], in_=wgt[:, HALF:J])
         for i in range(1, PACK):
             load_plane(0, i)
         for i in range(PACK):
             load_plane(1, i)
             load_scale_rows(wk_sc, wk_scales, i)
             load_scale_rows(wv4_sc, wv4_scales, i)
-        nc.sync.dma_start(
-            out=wk_codes[:].bitcast(I32), in_=wk_words.rearrange("a p n i -> p a (n i)").bitcast(I32)
-        )
-        nc.sync.dma_start(
-            out=wv4_codes[:].bitcast(I32), in_=wv4_words.rearrange("a p m -> p a m").bitcast(I32)
-        )
-        for a in range(PASSES):
-            nc.sync.dma_start(
-                out=wvd_raw[a][:],
-                in_=wvd[a * K_PASS : (a + 1) * K_PASS, :].rearrange("(p i) n -> p i n", i=PACK),
-            )
-        for h in range(HALVES):
-            for u in range(2):
-                nc.sync.dma_start(
-                    out=st_sb[h][u][:],
-                    in_=st[u * 2 * P : (u + 1) * 2 * P, h * HALF : (h + 1) * HALF].rearrange("(v p) j -> p v j", p=P),
-                )
+        nc.sync.dma_start(out=wk_codes[:].bitcast(I32), in_=wk_words.rearrange("a p n i -> p a (n i)").bitcast(I32))
+        nc.sync.dma_start(out=wv4_codes[:].bitcast(I32), in_=wv4_words.rearrange("a p m -> p a m").bitcast(I32))
+        load_wvd(0)
+        load_wvd(1)
+        load_st(0, 0)
+        load_st(0, 1)
+        load_st(1, 0)
+        load_st(1, 1)
 
         grouped = {}
         quantised = {}
         for key in ("x00", "x01", "x10", "x11", "w0", "w1"):
-            grouped[key] = keep.tile([P, HALF, PACK], BF16, name=f"grouped_{key}", align_bytes=64)
+            grouped[key] = keep.tile([P, HALF, PACK], BF16, name=f"grouped_{key}", align_bytes=64)[:]
+        grouped["w0"] = picked[1, 1][:, 3 * HALF : 5 * HALF].bitcast(BF16).rearrange("p (w t) -> p w t", t=PACK)
 
         def gather(a, i, h):
             nc.vector.tensor_tensor(
@@ -118,7 +136,7 @@ def tile_list_dl_silu_kernel(
             codes = keep.tile([P, HALF], U32, name=f"codes_{key}", align_bytes=64)
             scales = keep.tile([P, HALF], U8, name=f"scales_{key}", align_bytes=64)
             nc.vector.quantize_mx(
-                out=codes[:].bitcast(FP8X4), scales=scales[:], in_=grouped[key][:].rearrange("p w t -> p (w t)")
+                out=codes[:].bitcast(FP8X4), scales=scales[:], in_=grouped[key].rearrange("p w t -> p (w t)")
             )
             quantised[key] = (codes, scales)
 
@@ -139,13 +157,13 @@ def tile_list_dl_silu_kernel(
         gather(1, 1, 1)
         weave(1, 1, 0, 2)
         gather(1, 2, 1)
-        gather(1, 3, 1)
-        weave(1, 1, 2, 4)
-        interleave(nc.vector.tensor_copy, grouped["w0"][:], wvd_raw[0][:])
+        interleave(nc.vector.tensor_copy, grouped["w0"], wvd_raw[0])
         quantise("w0")
-        quantise("x11")
-        interleave(nc.scalar.copy, grouped["w1"][:], wvd_raw[1][:])
+        gather(1, 3, 1)
+        interleave(nc.scalar.copy, grouped["w1"], wvd_raw[1])
         quantise("w1")
+        weave(1, 1, 2, 4)
+        quantise("x11")
 
         def bank(b):
             return psum.tile([P, HALF], F32, name=f"bank{b}")
@@ -173,9 +191,12 @@ def tile_list_dl_silu_kernel(
             return gate
 
         def finish(ve, gate, t, h):
-            res = ring.tile([P, HALF], F32, name="res")
-            nc.vector.tensor_tensor(res[:], ve[:], gate[:], MULT)
-            nc.sync.dma_start(out=out[t * P : (t + 1) * P, h * HALF : (h + 1) * HALF], in_=res[:])
+            pieces = 2 if (t, h) == (N_TILES - 1, HALVES - 1) else 1
+            width = HALF // pieces
+            for c in range(0, HALF, width):
+                res = ring.tile([P, width], F32, name="res", bufs=6)
+                nc.vector.tensor_tensor(res[:], ve[:, c : c + width], gate[:, c : c + width], MULT)
+                nc.sync.dma_start(out=out[t * P : (t + 1) * P, h * HALF + c : h * HALF + c + width], in_=res[:])
 
         tiles = range(N_TILES)
         ke0 = [bank(t) for t in tiles]

@@ -81,7 +81,6 @@ def tile_list_dl_silu_kernel(
                 in_=st[u * 2 * P : (u + 1) * 2 * P, h * HALF : (h + 1) * HALF].rearrange("(v p) j -> p v j", p=P),
             )
 
-        nc.sync.dma_start(offsets[:], offs)
         rows = keep.tile([P, 64], F32, name="wgt_rows", align_bytes=64)
         for q in range(4):
             nc.sync.dma_start(
@@ -93,12 +92,13 @@ def tile_list_dl_silu_kernel(
             nc.vector.transpose(turned[:, 32 * u : 32 * (u + 1)], rows[:, 32 * u : 32 * (u + 1)])
         for h in range(HALVES):
             spread = keep.tile([P, HALF], F32, name=f"wgt_spread{h}", align_bytes=64)
-            nc.vector.tensor_copy(
+            (nc.vector.tensor_copy, nc.scalar.copy)[h](
                 out=spread[:].rearrange("p (b u r) -> p b u r", u=2, r=16),
                 in_=turned[:].rearrange("p (u b) -> p b u", u=2)[:, 16 * h : 16 * (h + 1), :].unsqueeze(3).to_broadcast([P, 16, 2, 16]),
             )
             nc.vector.transpose(wgt_sb[h], spread[:])
         load_plane(0, 0)
+        nc.sync.dma_start(offsets[:], offs)
         for i in range(1, PACK):
             load_plane(0, i)
         for i in range(PACK):
@@ -196,7 +196,7 @@ def tile_list_dl_silu_kernel(
             for c in range(0, HALF, width):
                 res = ring.tile([P, width], F32, name="res", bufs=6)
                 nc.vector.tensor_tensor(res[:], ve[:, c : c + width], gate[:, c : c + width], MULT)
-                nc.sync.dma_start(out=out[t * P : (t + 1) * P, h * HALF + c : h * HALF + c + width], in_=res[:])
+                (nc.scalar if pieces > 1 else nc.sync).dma_start(out=out[t * P : (t + 1) * P, h * HALF + c : h * HALF + c + width], in_=res[:])
 
         tiles = range(N_TILES)
         ke0 = [bank(t) for t in tiles]
@@ -218,8 +218,8 @@ def tile_list_dl_silu_kernel(
                 product(ke1[t], "wk", t, a, 1, a == 0, a == 1)
         ve1 = [bank(t) for t in tiles]
         for t in tiles:
-            for which in ("wv4", "wvd"):
-                for a in range(PASSES):
+            for a in range(PASSES):
+                for which in ("wv4", "wvd"):
                     product(ve1[t], which, t, a, 1, which == "wv4" and a == 0, which == "wvd" and a == 1)
         gates1 = [make_gate(ke1[t], t, 1) for t in tiles]
         for t in tiles:

from contextlib import ExitStack

import concourse.mybir as mybir

K, N, T, J = 1024, 512, 2048, 1024
FLOPS = 3 * 2 * K * N * J

F32 = mybir.dt.float32
BF16 = mybir.dt.bfloat16
I32 = mybir.dt.int32
U32 = mybir.dt.uint32
U16 = mybir.dt.uint16
U8 = mybir.dt.uint8
FP8X4 = mybir.dt.float8_e4m3fn_x4
FP4X4 = mybir.dt.float4_e2m1fn_x4
MULT = mybir.AluOpType.mult
SILU = mybir.ActivationFunctionType.Silu

P = 128
PACK = 4
K_PASS = P * PACK
PASSES = K // K_PASS
HALF = 512
HALVES = J // HALF
N_TILES = N // P
LIST_COLS = HALF // 16


def interleave(copy, grouped, rows):
    copy(
        out=grouped.rearrange("p (c i) t -> p c t i", i=4),
        in_=rows.rearrange("p t (c i) -> p c t i", i=4),
    )


def tile_list_dl_silu_kernel(
    tc, xT, wgt, wk_words, wk_scales, wv4_words, wv4_scales, wvd, st, offs, out
):
    nc = tc.nc
    with ExitStack() as ctx:
        keep = ctx.enter_context(tc.tile_pool(name="keep", bufs=1))
        ring = ctx.enter_context(tc.tile_pool(name="ring", bufs=4))
        psum = ctx.enter_context(tc.psum_pool(name="psum", bufs=1))

        offsets = keep.tile([P, J // 16], U16, name="offsets")
        picked = {(a, h): keep.tile([P, 2560 if (a, h) == (1, 1) else PACK * HALF], F32, name=f"picked{a}{h}", align_bytes=64) for a in range(PASSES) for h in range(HALVES)}
        wgt1 = keep.tile([P, HALF], F32, name="wgt1", align_bytes=64)
        wgt_sb = [picked[1, 1][:, 3 * HALF // 2 : 5 * HALF // 2], wgt1[:]]
        planes = [[keep.tile([P, T], F32, name=f"x{a}{i}") for i in range(PACK)] for a in range(PASSES)]
        wk_codes = keep.tile([P, PASSES, N], U32, name="wk_codes", align_bytes=64)
        wv4_codes = keep.tile([P, PASSES, 2 * N], U8, name="wv4_codes", align_bytes=64)
        wk_sc = keep.tile([P, PASSES, N], U8, name="wk_sc", align_bytes=64)
        wv4_sc = keep.tile([P, PASSES, N], U8, name="wv4_sc", align_bytes=64)
        wvd_raw = [keep.tile([P, PACK, N], F32, name=f"wvd_raw{a}")[:] for a in range(PASSES)]
        st_sb = [[keep.tile([P, 2, HALF], F32, name=f"st{h}{u}") for u in range(2)] for h in range(HALVES)]

        warm = keep.tile([P, 2], F32, name="warm")
        nc.vector.memset(warm[:, 0:1], 0.0)
        nc.scalar.activation(out=warm[:, 1:2], in_=warm[:, 0:1], func=SILU)
        for plane in (wk_sc, wv4_sc):
            nc.vector.memset(plane[:].rearrange("p a n -> p (a n)").bitcast(I32), 0)

        def load_plane(a, i):
            nc.sync.dma_start(out=planes[a][i][:], in_=xT[a * K_PASS + i : (a + 1) * K_PASS : PACK, :])

        def load_scale_rows(plane, scales, r):
            nc.sync.dma_start(
                out=plane[r:P:32, :, :].bitcast(I32),
                in_=scales[:, r:16:4, :].rearrange("a q n -> q a n").bitcast(I32),
            )

        def load_wvd(a):
            nc.sync.dma_start(
                out=wvd_raw[a],
                in_=wvd[a * K_PASS : (a + 1) * K_PASS, :].rearrange("(p i) n -> p i n", i=PACK),
            )

        def load_st(h, u):
            nc.sync.dma_start(
                out=st_sb[h][u][:],
                in_=st[u * 2 * P : (u + 1) * 2 * P, h * HALF : (h + 1) * HALF].rearrange("(v p) j -> p v j", p=P),
            )

        rows = keep.tile([P, 64], F32, name="wgt_rows", align_bytes=64)
        for q in range(4):
            nc.sync.dma_start(
                out=rows[32 * q : 32 * (q + 1), :].rearrange("b (u c) -> b u c", u=2),
                in_=wgt[32 * q : 32 * (q + 1) : 16, :].rearrange("u (b c) -> b u c", c=32),
            )
        turned = keep.tile([P, 64], F32, name="wgt_turned", align_bytes=64)
        for u in range(2):
            nc.vector.transpose(turned[:, 32 * u : 32 * (u + 1)], rows[:, 32 * u : 32 * (u + 1)])
        for h in range(HALVES):
            spread = keep.tile([P, HALF], F32, name=f"wgt_spread{h}", align_bytes=64)
            (nc.vector.tensor_copy, nc.scalar.copy)[h](
                out=spread[:].rearrange("p (b u r) -> p b u r", u=2, r=16),
                in_=turned[:].rearrange("p (u b) -> p b u", u=2)[:, 16 * h : 16 * (h + 1), :].unsqueeze(3).to_broadcast([P, 16, 2, 16]),
            )
            nc.vector.transpose(wgt_sb[h], spread[:])
        load_plane(0, 0)
        nc.sync.dma_start(offsets[:], offs)
        for i in range(1, PACK):
            load_plane(0, i)
        for i in range(PACK):
            load_plane(1, i)
            load_scale_rows(wk_sc, wk_scales, i)
            load_scale_rows(wv4_sc, wv4_scales, i)
        nc.sync.dma_start(out=wk_codes[:].bitcast(I32), in_=wk_words.rearrange("a p n i -> p a (n i)").bitcast(I32))
        nc.sync.dma_start(out=wv4_codes[:].bitcast(I32), in_=wv4_words.rearrange("a p m -> p a m").bitcast(I32))
        load_wvd(0)
        load_wvd(1)
        load_st(0, 0)
        load_st(0, 1)
        load_st(1, 0)
        load_st(1, 1)

        grouped = {}
        quantised = {}
        for key in ("x00", "x01", "x10", "x11", "w0", "w1"):
            grouped[key] = keep.tile([P, HALF, PACK], BF16, name=f"grouped_{key}", align_bytes=64)[:]
        grouped["w0"] = picked[1, 1][:, 3 * HALF : 5 * HALF].bitcast(BF16).rearrange("p (w t) -> p w t", t=PACK)

        def gather(a, i, h):
            nc.vector.tensor_tensor(
                picked[a, h][:, i * HALF : (i + 1) * HALF],
                planes[a][i][:].indirect(offsets[:, h * LIST_COLS : (h + 1) * LIST_COLS]),
                wgt_sb[h],
                MULT,
            )

        def weave(a, h, first, last):
            rows = picked[a, h][:, first * HALF : last * HALF].rearrange("p (t j) -> p t j", j=HALF)
            interleave(nc.scalar.copy, grouped[f"x{a}{h}"][:, :, first:last], rows)

        def quantise(key):
            codes = keep.tile([P, HALF], U32, name=f"codes_{key}", align_bytes=64)
            scales = keep.tile([P, HALF], U8, name=f"scales_{key}", align_bytes=64)
            nc.vector.quantize_mx(
                out=codes[:].bitcast(FP8X4), scales=scales[:], in_=grouped[key].rearrange("p w t -> p (w t)")
            )
            quantised[key] = (codes, scales)

        for i in range(PACK):
            for h in range(HALVES):
                gather(0, i, h)
        for h in range(HALVES):
            weave(0, h, 0, 4)
            quantise(f"x0{h}")
        gather(1, 0, 0)
        gather(1, 0, 1)
        gather(1, 1, 0)
        weave(1, 0, 0, 2)
        gather(1, 2, 0)
        gather(1, 3, 0)
        weave(1, 0, 2, 4)
        quantise("x10")
        gather(1, 1, 1)
        weave(1, 1, 0, 2)
        gather(1, 2, 1)
        interleave(nc.vector.tensor_copy, grouped["w0"], wvd_raw[0])
        quantise("w0")
        gather(1, 3, 1)
        interleave(nc.scalar.copy, grouped["w1"], wvd_raw[1])
        quantise("w1")
        weave(1, 1, 2, 4)
        quantise("x11")

        def bank(b):
            return psum.tile([P, HALF], F32, name=f"bank{b}")

        def product(acc, which, t, a, h, start, stop):
            cols = slice(t * P, (t + 1) * P)
            if which == "wk":
                codes, scales = wk_codes[:, a, cols].bitcast(FP8X4), wk_sc[:, a, cols]
            elif which == "wv4":
                codes, scales = wv4_codes[:, a, 2 * t * P : 2 * (t + 1) * P].bitcast(FP4X4), wv4_sc[:, a, cols]
            else:
                codes, scales = quantised[f"w{a}"][0][:, cols].bitcast(FP8X4), quantised[f"w{a}"][1][:, cols]
            x_codes, x_scales = quantised[f"x{a}{h}"]
            nc.tensor.matmul_mx(
                out=acc[:], lhsT=codes, lhsT_scale=scales,
                rhs=x_codes[:].bitcast(FP8X4), rhs_scale=x_scales[:],
                start=start, stop=stop,
            )

        def make_gate(ke, t, h):
            arg = ring.tile([P, HALF], F32, name="arg")
            nc.vector.tensor_tensor(arg[:], ke[:], st_sb[h][t // 2][:, t % 2, :], MULT)
            gate = ring.tile([P, HALF], F32, name="gate")
            nc.scalar.activation(out=gate[:], in_=arg[:], func=SILU)
            return gate

        def finish(ve, gate, t, h):
            pieces = 2 if (t, h) == (N_TILES - 1, HALVES - 1) else 1
            width = HALF // pieces
            for c in range(0, HALF, width):
                res = ring.tile([P, width], F32, name="res", bufs=6)
                nc.vector.tensor_tensor(res[:], ve[:, c : c + width], gate[:, c : c + width], MULT)
                (nc.scalar if pieces > 1 else nc.sync).dma_start(out=out[t * P : (t + 1) * P, h * HALF + c : h * HALF + c + width], in_=res[:])

        tiles = range(N_TILES)
        ke0 = [bank(t) for t in tiles]
        ve0 = [bank(N_TILES + t) for t in tiles]
        for a in range(PASSES):
            for t in tiles:
                product(ke0[t], "wk", t, a, 0, a == 0, a == 1)
            for t in tiles:
                product(ve0[t], "wv4", t, a, 0, a == 0, False)
        for a in range(PASSES):
            for t in tiles:
                product(ve0[t], "wvd", t, a, 0, False, a == 1)
        gates0 = [make_gate(ke0[t], t, 0) for t in tiles]
        ke1 = []
        for t in tiles:
            finish(ve0[t], gates0[t], t, 0)
            ke1.append(bank(N_TILES + t))
            for a in range(PASSES):
                product(ke1[t], "wk", t, a, 1, a == 0, a == 1)
        ve1 = [bank(t) for t in tiles]
        for t in tiles:
            for a in range(PASSES):
                for which in ("wv4", "wvd"):
                    product(ve1[t], which, t, a, 1, which == "wv4" and a == 0, which == "wvd" and a == 1)
        gates1 = [make_gate(ke1[t], t, 1) for t in tiles]
        for t in tiles:
            finish(ve1[t], gates1[t], t, 1)
